import numpy as np
import ml_dtypes


def mxq(x, axis, fmt="e4m3"):
    dtype, down = {"e4m3": (ml_dtypes.float8_e4m3fn, 7), "e5m2": (ml_dtypes.float8_e5m2, 14)}[fmt]
    v = np.moveaxis(np.asarray(x, np.float32).astype(ml_dtypes.bfloat16).astype(np.float64), axis, -1)
    blocks = v.reshape(v.shape[:-1] + (-1, 32))
    amax = np.abs(blocks).max(-1, keepdims=True)
    byte = np.maximum(np.where(amax > 0, np.frexp(amax)[1] - 1 + 127, 0) - down, 1)
    scale = np.exp2(byte - 127.0)
    codes = (blocks / scale).astype(np.float32).astype(dtype).astype(np.float64)
    return np.moveaxis((codes * scale).reshape(v.shape), -1, axis)


WIDE = False


def mx_kscale(k):
    if not WIDE:
        return np.ones(k)
    levels = np.array([10, -10, 5, -5, 0])
    if k % 512:
        return np.exp2(np.random.permutation(np.resize(levels, k // 32))).repeat(32)
    a = np.empty((k // 512, 16))
    for p in range(k // 512):
        a[p, :8] = np.random.permutation(np.resize(levels, 8))
        for g in range(8):
            far = levels[np.abs(levels - a[p, g]) >= 10]
            a[p, g + 8] = far[np.random.randint(len(far))]
    return np.exp2(a.ravel()).repeat(32)


def f64(x):
    return np.asarray(x).astype(np.float64)


def striped(idx):
    return np.tile(np.asarray(idx).reshape(-1, 16).T, (8, 1)).astype(np.uint16)


def unstriped(offs):
    return offs[:16].T.reshape(-1).astype(np.int64)


E2M1 = np.array([0.0, 0.5, 1.0, 1.5, 2.0, 3.0, 4.0, 6.0, -0.0, -0.5, -1.0, -1.5, -2.0, -3.0, -4.0, -6.0])


def pack_weight(w, fmt):
    k, n = w.shape
    w = f64(np.asarray(w, np.float32).astype(ml_dtypes.bfloat16)).reshape(k // 32, 32, n)
    amax = np.abs(w).max(1)
    if fmt == "e4m3":
        byte = np.frexp(amax)[1] - 1 + 127 - 7
    else:
        mant, ex = np.frexp(amax / 6.0)
        byte = np.where(mant > 0.5, ex, ex - 1) + 127
    byte = np.clip(np.where(amax > 0, byte, 1), 1, 254)
    scaled = (w * np.exp2(127.0 - byte)[:, None, :]).reshape(k, n).astype(np.float32)
    by_word = np.ascontiguousarray(scaled.reshape(k // 512, 128, 4, n).transpose(0, 1, 3, 2))
    if fmt == "e4m3":
        words = by_word.astype(ml_dtypes.float8_e4m3fn).view(np.uint8)
    else:
        c = by_word.astype(ml_dtypes.float4_e2m1fn).view(np.uint8) & 0xF
        words = (c[..., 0::2] | (c[..., 1::2] << 4)).reshape(k // 512, 128, 2 * n)
    return np.ascontiguousarray(words), np.ascontiguousarray(byte.astype(np.uint8).reshape(k // 512, 16, n))


def unpack_weight(words, scales, fmt):
    g, _, n = scales.shape
    words = np.ascontiguousarray(words).reshape(g, 128, n, -1)
    if fmt == "e4m3":
        vals = words.view(ml_dtypes.float8_e4m3fn).astype(np.float64)
    else:
        nib = np.empty((g, 128, n, 4), np.uint8)
        nib[..., 0::2] = words & 0xF
        nib[..., 1::2] = words >> 4
        vals = E2M1[nib]
    vals = vals * np.repeat(np.exp2(scales.astype(np.float64) - 127.0), 8, axis=1)[..., None]
    return vals.transpose(0, 1, 3, 2).reshape(g * 512, n)


K, R, F, T, J, M = 512, 128, 512, 2048, 512, 256


def setup_inputs():
    n = np.random.standard_normal
    idx = np.random.permutation(T)[:J]
    idx2 = np.random.permutation(J)[:M]
    idx3 = np.random.permutation(J)[:M]
    fk = mx_kscale(K)
    ff = mx_kscale(F)
    tabp = pack_weight(n((K, T)) / fk[:, None], "e4m3")
    return {
        "tab_words": tabp[0],
        "tab_scales": tabp[1],
        "w1": (n((K, R)) * 1 / np.sqrt(K) * fk[:, None]).astype(np.float32),
        "soft": (np.random.uniform(0.5, 1.5, (R, 1))).astype(np.float32),
        "wo": (n((F, R)) * 1 / np.sqrt(F) * ff[:, None]).astype(np.float32),
        "dy": (n((F, M)) / ff[:, None]).astype(np.float32),
        "old": (0.5 * n((R, J))).astype(np.float32),
        "offs": striped(idx),
        "offs2": striped(idx2),
        "offs3": striped(idx3),
    }


def reference(tab_words, tab_scales, w1, soft, wo, dy, old, offs, offs2, offs3):
    idx = unstriped(offs)
    idx2 = unstriped(offs2)
    idx3 = unstriped(offs3)
    tabu = unpack_weight(tab_words, tab_scales, "e4m3")
    w1q = mxq(f64(w1), 0, "e4m3")
    tabidxg = tabu[:, idx]
    a = w1q.T @ tabidxg
    n2 = np.sqrt(np.square(a[:, idx2]) * np.square(a[:, idx3]) + f64(soft))
    woq = mxq(f64(wo), 0, "e4m3")
    dyq = mxq(f64(dy), 0, "e4m3")
    c0 = woq.T @ dyq
    dn2 = c0 * a[:, idx2] * a[:, idx3] / np.square(n2) * (-1.0)
    e1 = c0 / n2 * a[:, idx3]
    s1 = np.zeros((R, J))
    s1[:, idx2] = e1
    e2 = dn2 * 0.5 / np.sqrt(np.square(a[:, idx2]) * np.square(a[:, idx3]) + f64(soft)) * np.square(a[:, idx3]) * a[:, idx2] * 2.0
    s2 = np.zeros((R, J))
    s2[:, idx2] = e2
    e3 = c0 / n2 * a[:, idx2]
    s3 = np.zeros((R, J))
    s3[:, idx3] = e3
    e4 = dn2 * 0.5 / np.sqrt(np.square(a[:, idx2]) * np.square(a[:, idx3]) + f64(soft)) * np.square(a[:, idx2]) * a[:, idx3] * 2.0
    s4 = np.zeros((R, J))
    s4[:, idx3] = e4
    da = s1 + s2 + s3 + s4
    y = da + f64(old)
    return y

@@ -1,0 +1,213 @@
+from contextlib import ExitStack
+
+import concourse.mybir as mybir
+
+K, R, F, T, J, M = 512, 128, 512, 2048, 512, 256
+FLOPS = 2 * K * R * J + 2 * F * R * M
+
+F32 = mybir.dt.float32
+BF16 = mybir.dt.bfloat16
+I32 = mybir.dt.int32
+U32 = mybir.dt.uint32
+U16 = mybir.dt.uint16
+U8 = mybir.dt.uint8
+FP8X4 = mybir.dt.float8_e4m3fn_x4
+ACT = mybir.ActivationFunctionType
+MULT = mybir.AluOpType.mult
+ADD = mybir.AluOpType.add
+
+P = 128
+PACK = 4
+LANES = 16
+HALVES = 2
+
+
+def tile_attend_clikeness_kernel(tc, tab_words, tab_scales, w1, soft, wo, dy, old, offs, offs2, offs3, out):
+    nc = tc.nc
+    with ExitStack() as ctx:
+        sb = ctx.enter_context(tc.tile_pool(name="sb", bufs=1))
+        ps = ctx.enter_context(tc.psum_pool(name="ps", bufs=1))
+
+        def tile(name, width, dtype):
+            return sb.tile([P, width], dtype, name=name, align_bytes=64)
+
+        slots = sb.tile([P, J // LANES], U16, name="slots")
+        first = sb.tile([P, M // LANES], U16, name="first")
+        second = sb.tile([P, M // LANES], U16, name="second")
+
+        table_scales = tile("table_scales", T, U8)
+        table_words = tile("table_words", T, I32)
+        w1_raw = tile("w1_raw", PACK * R, F32)
+        wo_raw = tile("wo_raw", PACK * R, F32)
+        dy_raw = tile("dy_raw", PACK * M, F32)
+        old_sb = tile("old_sb", J, F32)
+        soft_sb = tile("soft_sb", 1, F32)
+
+        nc.vector.memset(table_scales[:].bitcast(I32), 0)
+
+        warm_in = tile("warm_in", 1, F32)
+        warm_out = tile("warm_out", 1, F32)
+        nc.gpsimd.memset(warm_in[:], 1.0)
+        nc.scalar.activation(warm_out[:], warm_in[:], ACT.Abs_reciprocal_sqrt)
+
+        nc.sync.dma_start(out=w1_raw[:], in_=w1.rearrange("(p t) r -> p (t r)", t=PACK))
+        nc.sync.dma_start(slots[:], offs)
+        nc.sync.dma_start(first[:], offs2)
+        for q in range(4):
+            nc.sync.dma_start(
+                out=table_scales[32 * q : 32 * q + 4, :].bitcast(I32),
+                in_=tab_scales[0, 4 * q : 4 * q + 4, :].bitcast(I32),
+            )
+        nc.sync.dma_start(out=table_words[:], in_=tab_words[0].rearrange("p c t -> p (c t)").bitcast(I32))
+        nc.sync.dma_start(out=wo_raw[:], in_=wo.rearrange("(p t) r -> p (t r)", t=PACK))
+        nc.sync.dma_start(out=dy_raw[:], in_=dy.rearrange("(p t) m -> p (t m)", t=PACK))
+        nc.sync.dma_start(second[:], offs3)
+        nc.sync.dma_start(out=soft_sb[:], in_=soft)
+        nc.sync.dma_start(out=old_sb[:], in_=old)
+
+        at_first = tile("at_first", J, F32)
+        at_second = tile("at_second", J, F32)
+        nc.gpsimd.memset(at_first[:], 0.0)
+        nc.gpsimd.memset(at_second[:], 0.0)
+
+        def interleave(copy, name, raw, cols):
+            width = cols.stop - cols.start
+            grouped = tile(name, PACK * width, BF16)
+            copy(
+                out=grouped[:].rearrange("p (c i t) -> p c t i", i=4, t=PACK),
+                in_=raw[:].rearrange("p (t w) -> p t w", t=PACK)[:, :, cols].rearrange("p t (c i) -> p c t i", i=4),
+            )
+            return grouped
+
+        def quantise(name, grouped, width):
+            codes = tile(name + "_codes", width, U32)
+            scales = tile(name + "_scales", width, U8)
+            nc.vector.quantize_mx(out=codes[:].bitcast(FP8X4), scales=scales[:], in_=grouped[:])
+            return codes, scales
+
+        w1_codes, w1_scales = quantise("w1", interleave(nc.vector.tensor_copy, "w1_grouped", w1_raw, slice(0, R)), R)
+
+        picked_scales = tile("picked_scales", J, U8)
+        picked_words = tile("picked_words", J, U32)
+        nc.vector.tensor_copy(picked_scales[:], table_scales[:].indirect(slots[:]))
+
+        jh = J // HALVES
+        a_banks = []
+        for h in range(HALVES):
+            cols = slice(h * jh, (h + 1) * jh)
+            nc.vector.tensor_copy(
+                picked_words[:, cols],
+                table_words[:].bitcast(U32).indirect(slots[:, h * jh // LANES : (h + 1) * jh // LANES]),
+            )
+            bank = ps.tile([P, jh], F32, name=f"a_bank{h}")
+            nc.tensor.matmul_mx(
+                out=bank[:],
+                lhsT=w1_codes[:].bitcast(FP8X4),
+                lhsT_scale=w1_scales[:],
+                rhs=picked_words[:, cols].bitcast(FP8X4),
+                rhs_scale=picked_scales[:, cols],
+                start=True,
+                stop=True,
+            )
+            a_banks.append(bank)
+
+        CH = [128,128]
+        edges = [sum(CH[:i]) for i in range(len(CH) + 1)]
+        pieces = [slice(edges[i], edges[i + 1]) for i in range(len(CH))]
+        mh = M // 2
+        wo_grouped = interleave(nc.scalar.copy, "wo_grouped", wo_raw, slice(0, R))
+        dy_grouped = [
+            interleave(nc.scalar.copy, f"dy_grouped{h}", dy_raw, slice(h * mh, (h + 1) * mh)) for h in range(2)
+        ]
+
+        a_sb = tile("a_sb", J, F32)
+        nc.vector.tensor_copy(out=a_sb[:, 0:jh], in_=a_banks[0][:])
+        wo_codes, wo_scales = quantise("wo", wo_grouped, R)
+        nc.vector.tensor_copy(out=a_sb[:, jh:J], in_=a_banks[1][:])
+
+        def lanes(c):
+            return slice(c.start // LANES, c.stop // LANES)
+
+        x = tile("x", M, F32)
+        y = tile("y", M, F32)
+        prod = tile("prod", M, F32)
+        square = tile("square", M, F32)
+        root = tile("root", M, F32)
+        root2 = tile("root2", M, F32)
+        partt = tile("partt", M, F32)
+        gaint = tile("gaint", M, F32)
+        c_banks = [ps.tile([P, mh], F32, name=f"c_bank{h}") for h in range(2)]
+
+        def gx(c):
+            nc.vector.tensor_copy(x[:, c], a_sb[:].indirect(first[:, lanes(c)]))
+
+        def gy(c):
+            nc.vector.tensor_copy(y[:, c], a_sb[:].indirect(second[:, lanes(c)]))
+
+        def cq(h):
+            codes, scales = quantise(f"dy{h}", dy_grouped[h], mh)
+            nc.tensor.matmul_mx(
+                out=c_banks[h][:],
+                lhsT=wo_codes[:].bitcast(FP8X4),
+                lhsT_scale=wo_scales[:],
+                rhs=codes[:].bitcast(FP8X4),
+                rhs_scale=scales[:],
+                start=True,
+                stop=True,
+            )
+
+        def pr(c):
+            nc.vector.tensor_tensor(prod[:, c], x[:, c], y[:, c], MULT)
+
+        def sq(c):
+            nc.scalar.activation(square[:, c], prod[:, c], ACT.Square)
+
+        def rs(c):
+            nc.scalar.activation(root[:, c], square[:, c], ACT.Abs_reciprocal_sqrt, bias=soft_sb[:])
+
+        def r2(c):
+            nc.scalar.activation(root2[:, c], root[:, c], ACT.Square)
+
+        def part(c):
+            h = c.start // mh
+            nc.vector.scalar_tensor_tensor(partt[:, c], root[:, c], soft_sb[:], c_banks[h][:, c.start - h * mh : c.stop - h * mh], MULT, MULT)
+
+        def gain(c):
+            nc.vector.tensor_tensor(gaint[:, c], partt[:, c], root2[:, c], MULT)
+
+        def pf(c):
+            nc.vector.tensor_tensor(at_first[:].indirect(first[:, lanes(c)]), gaint[:, c], y[:, c], MULT)
+
+        def psn(c):
+            nc.vector.tensor_tensor(at_second[:].indirect(second[:, lanes(c)]), gaint[:, c], x[:, c], MULT)
+
+        whole = slice(0, M)
+        a, b = pieces
+        gx(whole)
+        gy(whole)
+        cq(0)
+        pr(a)
+        pr(b)
+        cq(1)
+        sq(a)
+        sq(b)
+        rs(a)
+        rs(b)
+        r2(a)
+        r2(b)
+        part(a)
+        part(b)
+        gain(a)
+        gain(b)
+        pf(whole)
+        psn(whole)
+
+        partial = tile("partial", J, F32)
+        total = [tile(f"total{h}", jh, F32) for h in range(HALVES)]
+        for h in range(HALVES):
+            cols = slice(h * jh, (h + 1) * jh)
+            nc.vector.tensor_tensor(partial[:, cols], at_first[:, cols], old_sb[:, cols], ADD)
+        for h in range(HALVES):
+            cols = slice(h * jh, (h + 1) * jh)
+            nc.vector.tensor_tensor(total[h][:], partial[:, cols], at_second[:, cols], ADD)
+            nc.sync.dma_start(out=out[:, cols], in_=total[h][:])

@@ -47,7 +47,7 @@ def tile_attend_clikeness_kernel(tc, tab_words, tab_scales, w1, soft, wo, dy, ol
 
         warm_in = tile("warm_in", 1, F32)
         warm_out = tile("warm_out", 1, F32)
-        nc.gpsimd.memset(warm_in[:], 1.0)
+        nc.vector.memset(warm_in[:], 1.0)
         nc.scalar.activation(warm_out[:], warm_in[:], ACT.Abs_reciprocal_sqrt)
 
         nc.sync.dma_start(out=w1_raw[:], in_=w1.rearrange("(p t) r -> p (t r)", t=PACK))
@@ -67,8 +67,8 @@ def tile_attend_clikeness_kernel(tc, tab_words, tab_scales, w1, soft, wo, dy, ol
 
         at_first = tile("at_first", J, F32)
         at_second = tile("at_second", J, F32)
-        nc.gpsimd.memset(at_first[:], 0.0)
-        nc.gpsimd.memset(at_second[:], 0.0)
+        nc.vector.memset(at_first[:], 0.0)
+        nc.vector.memset(at_second[:], 0.0)
 
         def interleave(copy, name, raw, cols):
             width = cols.stop - cols.start
@@ -99,31 +99,34 @@ def tile_attend_clikeness_kernel(tc, tab_words, tab_scales, w1, soft, wo, dy, ol
                 picked_words[:, cols],
                 table_words[:].bitcast(U32).indirect(slots[:, h * jh // LANES : (h + 1) * jh // LANES]),
             )
-            bank = ps.tile([P, jh], F32, name=f"a_bank{h}")
-            nc.tensor.matmul_mx(
-                out=bank[:],
-                lhsT=w1_codes[:].bitcast(FP8X4),
-                lhsT_scale=w1_scales[:],
-                rhs=picked_words[:, cols].bitcast(FP8X4),
-                rhs_scale=picked_scales[:, cols],
-                start=True,
-                stop=True,
-            )
-            a_banks.append(bank)
+            for cols in ([cols] if h == 0 else [slice(jh, jh + jh // 2), slice(jh + jh // 2, J)]):
+                bank = ps.tile([P, cols.stop - cols.start], F32, name=f"a_bank{cols.start}")
+                nc.tensor.matmul_mx(
+                    out=bank[:],
+                    lhsT=w1_codes[:].bitcast(FP8X4),
+                    lhsT_scale=w1_scales[:],
+                    rhs=picked_words[:, cols].bitcast(FP8X4),
+                    rhs_scale=picked_scales[:, cols],
+                    start=True,
+                    stop=True,
+                )
+                a_banks.append(bank)
 
         CH = [128,128]
         edges = [sum(CH[:i]) for i in range(len(CH) + 1)]
         pieces = [slice(edges[i], edges[i + 1]) for i in range(len(CH))]
         mh = M // 2
         wo_grouped = interleave(nc.scalar.copy, "wo_grouped", wo_raw, slice(0, R))
-        dy_grouped = [
-            interleave(nc.scalar.copy, f"dy_grouped{h}", dy_raw, slice(h * mh, (h + 1) * mh)) for h in range(2)
-        ]
 
         a_sb = tile("a_sb", J, F32)
         nc.vector.tensor_copy(out=a_sb[:, 0:jh], in_=a_banks[0][:])
         wo_codes, wo_scales = quantise("wo", wo_grouped, R)
-        nc.vector.tensor_copy(out=a_sb[:, jh:J], in_=a_banks[1][:])
+        nc.vector.tensor_copy(out=a_sb[:, jh : jh + jh // 2], in_=a_banks[1][:])
+        nc.scalar.copy(out=a_sb[:, jh + jh // 2 : J], in_=a_banks[2][:])
+
+        dy_grouped = [
+            interleave(nc.scalar.copy, f"dy_grouped{h}", dy_raw, slice(h * mh, (h + 1) * mh)) for h in range(2)
+        ]
 
         def lanes(c):
             return slice(c.start // LANES, c.stop // LANES)
@@ -183,24 +186,28 @@ def tile_attend_clikeness_kernel(tc, tab_words, tab_scales, w1, soft, wo, dy, ol
 
         whole = slice(0, M)
         a, b = pieces
-        gx(whole)
-        gy(whole)
-        cq(0)
+        gx(a)
+        gy(a)
+        gx(b)
         pr(a)
-        pr(b)
-        cq(1)
         sq(a)
-        sq(b)
+        gy(b)
+        cq(0)
         rs(a)
-        rs(b)
+        pr(b)
+        sq(b)
+        cq(1)
         r2(a)
-        r2(b)
         part(a)
-        part(b)
+        rs(b)
         gain(a)
+        r2(b)
+        part(b)
+        pf(a)
         gain(b)
-        pf(whole)
-        psn(whole)
+        psn(a)
+        pf(b)
+        psn(b)
 
         partial = tile("partial", J, F32)
         total = [tile(f"total{h}", jh, F32) for h in range(HALVES)]

@@ -55,8 +55,8 @@ def tile_attend_clikeness_kernel(tc, tab_words, tab_scales, w1, soft, wo, dy, ol
         nc.sync.dma_start(first[:], offs2)
         for q in range(4):
             nc.sync.dma_start(
-                out=table_scales[32 * q : 32 * q + 4, :].bitcast(I32),
-                in_=tab_scales[0, 4 * q : 4 * q + 4, :].bitcast(I32),
+                out=table_scales[q:P:32, :].bitcast(I32),
+                in_=tab_scales[0, q:16:4, :].bitcast(I32),
             )
         nc.sync.dma_start(out=table_words[:], in_=tab_words[0].rearrange("p c t -> p (c t)").bitcast(I32))
         nc.sync.dma_start(out=wo_raw[:], in_=wo.rearrange("(p t) r -> p (t r)", t=PACK))

@@ -52,14 +52,16 @@ def tile_attend_clikeness_kernel(tc, tab_words, tab_scales, w1, soft, wo, dy, ol
 
         nc.sync.dma_start(out=w1_raw[:], in_=w1.rearrange("(p t) r -> p (t r)", t=PACK))
         nc.sync.dma_start(slots[:], offs)
-        nc.sync.dma_start(first[:], offs2)
+        words_hbm = tab_words[0].rearrange("p c t -> p (c t)").bitcast(I32)
+        nc.sync.dma_start(out=table_words[:, 0 : T // 4], in_=words_hbm[:, 0 : T // 4])
         for q in range(4):
             nc.sync.dma_start(
                 out=table_scales[q:P:32, :].bitcast(I32),
                 in_=tab_scales[0, q:16:4, :].bitcast(I32),
             )
-        nc.sync.dma_start(out=table_words[:], in_=tab_words[0].rearrange("p c t -> p (c t)").bitcast(I32))
+        nc.sync.dma_start(out=table_words[:, T // 4 : T], in_=words_hbm[:, T // 4 : T])
         nc.sync.dma_start(out=wo_raw[:], in_=wo.rearrange("(p t) r -> p (t r)", t=PACK))
+        nc.sync.dma_start(first[:], offs2)
         nc.sync.dma_start(out=dy_raw[:], in_=dy.rearrange("(p t) m -> p (t m)", t=PACK))
         nc.sync.dma_start(second[:], offs3)
         nc.sync.dma_start(out=soft_sb[:], in_=soft)

from contextlib import ExitStack

import concourse.mybir as mybir

K, R, F, T, J, M = 512, 128, 512, 2048, 512, 256
FLOPS = 2 * K * R * J + 2 * F * R * M

F32 = mybir.dt.float32
BF16 = mybir.dt.bfloat16
I32 = mybir.dt.int32
U32 = mybir.dt.uint32
U16 = mybir.dt.uint16
U8 = mybir.dt.uint8
FP8X4 = mybir.dt.float8_e4m3fn_x4
ACT = mybir.ActivationFunctionType
MULT = mybir.AluOpType.mult
ADD = mybir.AluOpType.add

P = 128
PACK = 4
LANES = 16
HALVES = 2


def tile_attend_clikeness_kernel(tc, tab_words, tab_scales, w1, soft, wo, dy, old, offs, offs2, offs3, out):
    nc = tc.nc
    with ExitStack() as ctx:
        sb = ctx.enter_context(tc.tile_pool(name="sb", bufs=1))
        ps = ctx.enter_context(tc.psum_pool(name="ps", bufs=1))

        def tile(name, width, dtype):
            return sb.tile([P, width], dtype, name=name, align_bytes=64)

        slots = sb.tile([P, J // LANES], U16, name="slots")
        first = sb.tile([P, M // LANES], U16, name="first")
        second = sb.tile([P, M // LANES], U16, name="second")

        table_scales = tile("table_scales", T, U8)
        table_words = tile("table_words", T, I32)
        w1_raw = tile("w1_raw", PACK * R, F32)
        wo_raw = tile("wo_raw", PACK * R, F32)
        dy_raw = tile("dy_raw", PACK * M, F32)
        old_sb = tile("old_sb", J, F32)
        soft_sb = tile("soft_sb", 1, F32)

        nc.vector.memset(table_scales[:].bitcast(I32), 0)

        warm_in = tile("warm_in", 1, F32)
        warm_out = tile("warm_out", 1, F32)
        nc.vector.memset(warm_in[:], 1.0)
        nc.scalar.activation(warm_out[:], warm_in[:], ACT.Abs_reciprocal_sqrt)

        nc.sync.dma_start(out=w1_raw[:], in_=w1.rearrange("(p t) r -> p (t r)", t=PACK))
        nc.sync.dma_start(slots[:], offs)
        words_hbm = tab_words[0].rearrange("p c t -> p (c t)").bitcast(I32)
        nc.sync.dma_start(out=table_words[:, 0 : T // 4], in_=words_hbm[:, 0 : T // 4])
        for q in range(4):
            nc.sync.dma_start(
                out=table_scales[q:P:32, :].bitcast(I32),
                in_=tab_scales[0, q:16:4, :].bitcast(I32),
            )
        nc.sync.dma_start(out=table_words[:, T // 4 : T], in_=words_hbm[:, T // 4 : T])
        nc.sync.dma_start(out=wo_raw[:], in_=wo.rearrange("(p t) r -> p (t r)", t=PACK))
        nc.sync.dma_start(first[:], offs2)
        nc.sync.dma_start(out=dy_raw[:], in_=dy.rearrange("(p t) m -> p (t m)", t=PACK))
        nc.sync.dma_start(second[:], offs3)
        nc.sync.dma_start(out=soft_sb[:], in_=soft)
        nc.sync.dma_start(out=old_sb[:], in_=old)

        at_first = tile("at_first", J, F32)
        at_second = tile("at_second", J, F32)
        nc.vector.memset(at_first[:], 0.0)
        nc.vector.memset(at_second[:], 0.0)

        def interleave(copy, name, raw, cols):
            width = cols.stop - cols.start
            grouped = tile(name, PACK * width, BF16)
            copy(
                out=grouped[:].rearrange("p (c i t) -> p c t i", i=4, t=PACK),
                in_=raw[:].rearrange("p (t w) -> p t w", t=PACK)[:, :, cols].rearrange("p t (c i) -> p c t i", i=4),
            )
            return grouped

        def quantise(name, grouped, width):
            codes = tile(name + "_codes", width, U32)
            scales = tile(name + "_scales", width, U8)
            nc.vector.quantize_mx(out=codes[:].bitcast(FP8X4), scales=scales[:], in_=grouped[:])
            return codes, scales

        w1_codes, w1_scales = quantise("w1", interleave(nc.vector.tensor_copy, "w1_grouped", w1_raw, slice(0, R)), R)

        picked_scales = tile("picked_scales", J, U8)
        picked_words = tile("picked_words", J, U32)
        nc.vector.tensor_copy(picked_scales[:], table_scales[:].indirect(slots[:]))

        jh = J // HALVES
        a_banks = []
        for h in range(HALVES):
            cols = slice(h * jh, (h + 1) * jh)
            nc.vector.tensor_copy(
                picked_words[:, cols],
                table_words[:].bitcast(U32).indirect(slots[:, h * jh // LANES : (h + 1) * jh // LANES]),
            )
            for cols in ([cols] if h == 0 else [slice(jh, jh + jh // 2), slice(jh + jh // 2, J)]):
                bank = ps.tile([P, cols.stop - cols.start], F32, name=f"a_bank{cols.start}")
                nc.tensor.matmul_mx(
                    out=bank[:],
                    lhsT=w1_codes[:].bitcast(FP8X4),
                    lhsT_scale=w1_scales[:],
                    rhs=picked_words[:, cols].bitcast(FP8X4),
                    rhs_scale=picked_scales[:, cols],
                    start=True,
                    stop=True,
                )
                a_banks.append(bank)

        CH = [128,128]
        edges = [sum(CH[:i]) for i in range(len(CH) + 1)]
        pieces = [slice(edges[i], edges[i + 1]) for i in range(len(CH))]
        mh = M // 2
        wo_grouped = interleave(nc.scalar.copy, "wo_grouped", wo_raw, slice(0, R))

        a_sb = tile("a_sb", J, F32)
        nc.vector.tensor_copy(out=a_sb[:, 0:jh], in_=a_banks[0][:])
        wo_codes, wo_scales = quantise("wo", wo_grouped, R)
        nc.vector.tensor_copy(out=a_sb[:, jh : jh + jh // 2], in_=a_banks[1][:])
        nc.scalar.copy(out=a_sb[:, jh + jh // 2 : J], in_=a_banks[2][:])

        dy_grouped = [
            interleave(nc.scalar.copy, f"dy_grouped{h}", dy_raw, slice(h * mh, (h + 1) * mh)) for h in range(2)
        ]

        def lanes(c):
            return slice(c.start // LANES, c.stop // LANES)

        x = tile("x", M, F32)
        y = tile("y", M, F32)
        prod = tile("prod", M, F32)
        square = tile("square", M, F32)
        root = tile("root", M, F32)
        root2 = tile("root2", M, F32)
        partt = tile("partt", M, F32)
        gaint = tile("gaint", M, F32)
        c_banks = [ps.tile([P, mh], F32, name=f"c_bank{h}") for h in range(2)]

        def gx(c):
            nc.vector.tensor_copy(x[:, c], a_sb[:].indirect(first[:, lanes(c)]))

        def gy(c):
            nc.vector.tensor_copy(y[:, c], a_sb[:].indirect(second[:, lanes(c)]))

        def cq(h):
            codes, scales = quantise(f"dy{h}", dy_grouped[h], mh)
            nc.tensor.matmul_mx(
                out=c_banks[h][:],
                lhsT=wo_codes[:].bitcast(FP8X4),
                lhsT_scale=wo_scales[:],
                rhs=codes[:].bitcast(FP8X4),
                rhs_scale=scales[:],
                start=True,
                stop=True,
            )

        def pr(c):
            nc.vector.tensor_tensor(prod[:, c], x[:, c], y[:, c], MULT)

        def sq(c):
            nc.scalar.activation(square[:, c], prod[:, c], ACT.Square)

        def rs(c):
            nc.scalar.activation(root[:, c], square[:, c], ACT.Abs_reciprocal_sqrt, bias=soft_sb[:])

        def r2(c):
            nc.scalar.activation(root2[:, c], root[:, c], ACT.Square)

        def part(c):
            h = c.start // mh
            nc.vector.scalar_tensor_tensor(partt[:, c], root[:, c], soft_sb[:], c_banks[h][:, c.start - h * mh : c.stop - h * mh], MULT, MULT)

        def gain(c):
            nc.vector.tensor_tensor(gaint[:, c], partt[:, c], root2[:, c], MULT)

        def pf(c):
            nc.vector.tensor_tensor(at_first[:].indirect(first[:, lanes(c)]), gaint[:, c], y[:, c], MULT)

        def psn(c):
            nc.vector.tensor_tensor(at_second[:].indirect(second[:, lanes(c)]), gaint[:, c], x[:, c], MULT)

        whole = slice(0, M)
        a, b = pieces
        gx(a)
        gy(a)
        gx(b)
        pr(a)
        sq(a)
        gy(b)
        cq(0)
        rs(a)
        pr(b)
        sq(b)
        cq(1)
        r2(a)
        part(a)
        rs(b)
        gain(a)
        r2(b)
        part(b)
        pf(a)
        gain(b)
        psn(a)
        pf(b)
        psn(b)

        partial = tile("partial", J, F32)
        total = [tile(f"total{h}", jh, F32) for h in range(HALVES)]
        for h in range(HALVES):
            cols = slice(h * jh, (h + 1) * jh)
            nc.vector.tensor_tensor(partial[:, cols], at_first[:, cols], old_sb[:, cols], ADD)
        for h in range(HALVES):
            cols = slice(h * jh, (h + 1) * jh)
            nc.vector.tensor_tensor(total[h][:], partial[:, cols], at_second[:, cols], ADD)
            nc.sync.dma_start(out=out[:, cols], in_=total[h][:])
